import numpy as np
import ml_dtypes


def mxq(x, axis, fmt="e4m3"):
    dtype, down = {"e4m3": (ml_dtypes.float8_e4m3fn, 7), "e5m2": (ml_dtypes.float8_e5m2, 14)}[fmt]
    v = np.moveaxis(np.asarray(x, np.float32).astype(ml_dtypes.bfloat16).astype(np.float64), axis, -1)
    blocks = v.reshape(v.shape[:-1] + (-1, 32))
    amax = np.abs(blocks).max(-1, keepdims=True)
    byte = np.maximum(np.where(amax > 0, np.frexp(amax)[1] - 1 + 127, 0) - down, 1)
    scale = np.exp2(byte - 127.0)
    codes = (blocks / scale).astype(np.float32).astype(dtype).astype(np.float64)
    return np.moveaxis((codes * scale).reshape(v.shape), -1, axis)


WIDE = False


def mx_kscale(k):
    if not WIDE:
        return np.ones(k)
    levels = np.array([10, -10, 5, -5, 0])
    if k % 512:
        return np.exp2(np.random.permutation(np.resize(levels, k // 32))).repeat(32)
    a = np.empty((k // 512, 16))
    for p in range(k // 512):
        a[p, :8] = np.random.permutation(np.resize(levels, 8))
        for g in range(8):
            far = levels[np.abs(levels - a[p, g]) >= 10]
            a[p, g + 8] = far[np.random.randint(len(far))]
    return np.exp2(a.ravel()).repeat(32)


def f64(x):
    return np.asarray(x).astype(np.float64)


def striped(idx):
    return np.tile(idx.reshape(-1, 16).T, (8, 1)).astype(np.uint16)


def unstriped(offs):
    return offs[:16].T.reshape(-1).astype(np.int64)


def striped8(idx):
    return np.concatenate([x.reshape(-1, 16).T for x in idx]).astype(np.uint16)


def runs(offs, k):
    lists = np.stack([offs[16 * r : 16 * r + 16].T.reshape(-1) for r in range(8)]).astype(np.int64)
    return lists[np.arange(k) % 512 // 64]


def pack_weight(w):
    k, n = w.shape
    w = f64(np.asarray(w, np.float32).astype(ml_dtypes.bfloat16)).reshape(k // 32, 32, n)
    amax = np.abs(w).max(1)
    byte = np.clip(np.where(amax > 0, np.frexp(amax)[1] - 1 + 127 - 7, 1), 1, 254)
    scaled = (w * np.exp2(127.0 - byte)[:, None, :]).reshape(k, n).astype(np.float32)
    words = np.ascontiguousarray(scaled.reshape(k // 512, 128, 4, n).transpose(0, 1, 3, 2)).astype(ml_dtypes.float8_e4m3fn).view(np.uint8)
    return words, np.ascontiguousarray(byte.astype(np.uint8).reshape(k // 512, 16, n))


def unpack_weight(words, scales):
    g, p, n, _ = words.shape
    vals = np.ascontiguousarray(words).view(ml_dtypes.float8_e4m3fn).astype(np.float64) * np.repeat(np.exp2(scales.astype(np.float64) - 127.0), 8, axis=1)[..., None]
    return vals.transpose(0, 1, 3, 2).reshape(g * 512, n)


def sigmoid(v):
    return 1.0 / (1.0 + np.exp(-np.maximum(v, -700.0)))

def planes(y):
    n, m = y.shape
    v = y.astype(np.float32).astype(ml_dtypes.bfloat16).astype(np.float64).reshape(n // 32, 32, m)
    top = np.abs(v).max(1)
    byte = np.clip(np.where(top > 0, np.frexp(top)[1] - 1 + 127 - 7, 1), 1, 254)
    codes = (v * np.exp2(127.0 - byte)[:, None, :]).reshape(n, m).astype(np.float32).astype(ml_dtypes.float8_e4m3fn).view(np.uint8)
    words = codes.reshape(n // 512, 128, 4, m).transpose(0, 1, 3, 2)
    return np.ascontiguousarray(words), np.ascontiguousarray(byte.astype(np.uint8).reshape(n // 512, 16, m))


K, T, S, N, G, H = 512, 2048, 512, 512, 2048, 512


def setup_inputs():
    n = np.random.standard_normal
    s = mx_kscale(K)[:, None]
    u = mx_kscale(S)
    packed_xT = pack_weight(n((K, T)) * s)
    packed_dT = pack_weight(n((K, G)) / s)
    packed_w1 = pack_weight(n((H, N)) / np.sqrt(H) / u[:, None])
    return {
        "x_words": packed_xT[0],
        "x_scales": packed_xT[1],
        "d_words": packed_dT[0],
        "d_scales": packed_dT[1],
        "gn": (np.random.uniform(0.5, 1.5, (H, 1)) * u[:, None]).astype(np.float32),
        "w1_words": packed_w1[0],
        "w1_scales": packed_w1[1],
        "offs": striped(np.random.permutation(T)[:S]),
        "k1": striped8(np.random.randint(0, G, (8, H))),
        "two": striped(np.random.permutation(T)[:S]),
        "n1": striped(np.random.permutation(S)),
        "n2": striped(np.random.permutation(S)),
        "n3": striped8(np.stack([np.random.permutation(S) for _ in range(8)])),
    }


def reference(x_words, x_scales, d_words, d_scales, gn, w1_words, w1_scales, offs, k1, two, n1, n2, n3):
    d_k1 = unpack_weight(d_words, d_scales)[np.arange(K)[:, None], runs(k1, K)]
    xq = unpack_weight(x_words, x_scales)[:, unstriped(offs)]
    a = 0.0625 * (d_k1.T @ xq)
    x_two = unpack_weight(x_words, x_scales)[:, unstriped(two)]
    b = 0.0625 * (d_k1.T @ x_two)
    z = f64(gn) * (a + (sigmoid(b[:, unstriped(n2)] - b)) * (a[:, unstriped(n1)] - a))
    h = unpack_weight(w1_words, w1_scales).T @ mxq(z, 0, "e4m3")
    out_0 = np.maximum(h, h[np.arange(N)[:, None], runs(n3, N)])
    return (out_0,) + planes(out_0)

@@ -1,0 +1,279 @@
+from contextlib import ExitStack
+
+import concourse.mybir as mybir
+
+K, T, S, N, G, H = 512, 2048, 512, 512, 2048, 512
+FLOPS = 2 * K * H * S * 2 + 2 * H * N * S
+
+F32 = mybir.dt.float32
+BF16 = mybir.dt.bfloat16
+I32 = mybir.dt.int32
+U32 = mybir.dt.uint32
+U16 = mybir.dt.uint16
+U8 = mybir.dt.uint8
+FP8X4 = mybir.dt.float8_e4m3fn_x4
+ACT = mybir.ActivationFunctionType
+ALU = mybir.AluOpType
+
+P = 128
+PACK = 4
+LIST_ROWS = 16
+SCORE_SCALE = 0.0625
+MIX_CHUNKS = ((0, 256), (256, 128), (384, 128))
+OUT_CHUNKS = ((0, 256), (256, 128), (384, 128))
+FETCH = 256
+B_ON_SCALAR = (0, 1, 2)
+A_ON_SCALAR = (0,)
+H_ON_SCALAR = (0, 1, 2, 3)
+GATE_BUFS = 4
+STEP_BUFS = 3
+OTHER_BUFS = 4
+LEAD = 2
+N1_ON_VECTOR = ((0, 1),)
+D_ZERO_GPSIMD = False
+FAR_BUFS = 2
+PIECE = 128
+ROW_TAGS = ("rows0", "rows1", "x_scale_table", "x_word_table")
+
+
+def entries(offsets, start, width):
+    return offsets[:, start // LIST_ROWS : (start + width) // LIST_ROWS]
+
+
+def words_in_hbm(words):
+    return words[0].rearrange("p n t -> p (n t)").bitcast(I32)
+
+
+def dealt_views(dst, src, run):
+    return (
+        dst.rearrange("p (t c i) -> p c t i", t=PACK, i=run),
+        src.rearrange("p (c i t) -> p c t i", t=PACK, i=run),
+    )
+
+
+def woven(tile, start, width):
+    return tile[:, PACK * start : PACK * (start + width)].rearrange("p (c i t) -> p c t i", t=PACK, i=PACK)
+
+
+def planar(tile, start, width):
+    return tile[:, :, start : start + width].rearrange("p t (c i) -> p c t i", i=PACK)
+
+
+def tile_picked_twkspullbbig_none_po_kernel(
+    tc, x_words, x_scales, d_words, d_scales, gn, w1_words, w1_scales, offs, k1, two, n1, n2, n3, out_0, out_1, out_2
+):
+    nc = tc.nc
+    with ExitStack() as ctx:
+        held = ctx.enter_context(tc.tile_pool(name="held", bufs=1))
+        ring = ctx.enter_context(tc.tile_pool(name="ring", bufs=3))
+        psum = ctx.enter_context(tc.psum_pool(name="psum", bufs=1))
+
+        def new(shape, dtype, name, tag=None):
+            return held.tile(shape, dtype, name=name, tag=tag or name, align_bytes=64)
+
+        def load_list(source, name):
+            offsets = new([P, S // LIST_ROWS], U16, name)
+            nc.sync.dma_start(offsets[:], source)
+            return offsets
+
+        d_scale_table = new([P, G], U8, "d_scale_table")
+        x_scale_table = new([P, T], U8, "x_scale_table")
+        d_word_table = new([P, G], U32, "d_word_table")
+        x_word_table = new([P, T], U32, "x_word_table")
+        key_scales = new([P, H], U8, "key_scales")
+        w_scales_raw = new([P, N], U8, "w_scales_raw")
+        w_words_raw = new([P, N], U32, "w_words_raw")
+        gain = new([P, PACK], F32, "gain")
+
+        (nc.gpsimd if D_ZERO_GPSIMD else nc.vector).memset(d_scale_table[:].bitcast(I32), 0)
+        nc.vector.memset(x_scale_table[:].bitcast(I32), 0)
+        nc.vector.memset(key_scales[:].bitcast(I32), 0)
+        nc.gpsimd.memset(w_scales_raw[:].bitcast(I32), 0)
+
+        k1_list = load_list(k1, "k1_list")
+        two_list = load_list(two, "two_list")
+        nc.sync.dma_start(d_scale_table[0:P:8, :].bitcast(I32), d_scales[0].bitcast(I32))
+        for q in range(4):
+            queue = nc.scalar if q < 2 else nc.sync
+            queue.dma_start(
+                x_scale_table[32 * q : 32 * q + 4, :].bitcast(I32), x_scales[0, 4 * q : 4 * q + 4, :].bitcast(I32)
+            )
+        nc.sync.dma_start(d_word_table[:].bitcast(I32), words_in_hbm(d_words))
+        nc.sync.dma_start(x_word_table[:].bitcast(I32), words_in_hbm(x_words))
+        n2_list = load_list(n2, "n2_list")
+        nc.gpsimd.dma_start(gain[:], gn.rearrange("(p t) o -> p (t o)", t=PACK))
+        for q in range(4):
+            nc.gpsimd.dma_start(
+                w_scales_raw[32 * q : 32 * q + 4, :].bitcast(I32), w1_scales[0, 4 * q : 4 * q + 4, :].bitcast(I32)
+            )
+
+        row_scale = new([P, PACK], F32, "row_scale")
+        nc.scalar.activation(row_scale[:], gain[:], ACT.Copy, scale=SCORE_SCALE / 2)
+
+        picked_d_scales = new([P, H], U8, "picked_d_scales")
+        dealt_d_scales = new([P, H], U8, "dealt_d_scales")
+        nc.vector.tensor_copy(picked_d_scales[:], d_scale_table[:].indirect(k1_list[:]))
+        nc.vector.tensor_copy(*dealt_views(dealt_d_scales[:], picked_d_scales[:], 16))
+        for r in range(4):
+            nc.sync.dma_start(key_scales[r:P:32, :].bitcast(I32), dealt_d_scales[8 * r : P : 32, :].bitcast(I32))
+        n1_list = load_list(n1, "n1_list")
+        offs_list = load_list(offs, "offs_list")
+        nc.sync.dma_start(w_words_raw[:].bitcast(I32), words_in_hbm(w1_words))
+        n3_list = load_list(n3, "n3_list")
+
+        two_scales = new([P, S], U8, "two_scales")
+        nc.vector.tensor_copy(two_scales[:], x_scale_table[:].indirect(two_list[:]))
+        picked_d_words = new([P, H], U32, "picked_d_words")
+        key_words = new([P, H], U32, "key_words")
+        nc.vector.tensor_copy(picked_d_words[:], d_word_table[:].indirect(k1_list[:]))
+        nc.vector.tensor_copy(*dealt_views(key_words[:], picked_d_words[:], 4))
+        two_words = new([P, S], U32, "two_words")
+        nc.vector.tensor_copy(two_words[:], x_word_table[:].indirect(two_list[:]))
+
+        def product(bank, lhs_words, lhs_scales, t, rhs_words, rhs_scales):
+            rows = slice(P * t, P * (t + 1))
+            nc.tensor.matmul_mx(
+                out=bank,
+                lhsT=lhs_words[:, rows].bitcast(FP8X4),
+                lhsT_scale=lhs_scales[:, rows],
+                rhs=rhs_words.bitcast(FP8X4),
+                rhs_scale=rhs_scales,
+                start=True,
+                stop=True,
+            )
+
+        b_banks = [psum.tile([P, S], F32, name="b_bank%d" % t, tag="low%d" % t) for t in range(PACK)]
+        for t in range(PACK):
+            product(b_banks[t][:], key_words, key_scales, t, two_words[:], two_scales[:])
+
+        offs_scales = new([P, S], U8, "offs_scales")
+        offs_words = new([P, S], U32, "offs_words")
+        nc.vector.tensor_copy(offs_scales[:], x_scale_table[:].indirect(offs_list[:]))
+        nc.vector.tensor_copy(offs_words[:], x_word_table[:].indirect(offs_list[:]))
+        a_banks = [psum.tile([P, S], F32, name="a_bank%d" % t, tag="high%d" % t) for t in range(PACK)]
+        for t in range(PACK):
+            product(a_banks[t][:], key_words, key_scales, t, offs_words[:], offs_scales[:])
+
+        w_words = new([P, N], U32, "w_words")
+        w_scales = new([P, N], U8, "w_scales")
+        nc.gpsimd.tensor_copy(*dealt_views(w_words[:], w_words_raw[:], 4))
+        nc.gpsimd.tensor_copy(*dealt_views(w_scales[:], w_scales_raw[:], 16))
+
+        b_rows = [new([P, S], F32, "b_rows%d" % t, ROW_TAGS[t]) for t in range(PACK)]
+        a_rows = [new([P, S], F32, "a_rows%d" % t) for t in range(PACK)]
+        far = new([P, PACK, S], F32, "far")
+        near = new([P, PACK, S], F32, "near")
+        z_woven = new([P, PACK * S], BF16, "z_woven")
+        z_words = new([P, S], U32, "z_words")
+        z_scales = new([P, S], U8, "z_scales")
+        h_banks = [psum.tile([P, S], F32, name="h_bank%d" % t, tag="low%d" % t) for t in range(PACK)]
+
+        def leave_b(t):
+            if t in B_ON_SCALAR:
+                nc.scalar.copy(b_rows[t][:], b_banks[t][:])
+            else:
+                nc.vector.tensor_copy(b_rows[t][:], b_banks[t][:])
+
+        def leave_a(t):
+            if t in A_ON_SCALAR:
+                nc.scalar.activation(a_rows[t][:], a_banks[t][:], ACT.Copy, scale=row_scale[:, t : t + 1])
+            else:
+                nc.vector.tensor_scalar(a_rows[t][:], a_banks[t][:], row_scale[:, t : t + 1], None, ALU.mult)
+
+        def fetch(out, window, offsets, start, width, on_vector):
+            for lo in range(0, width, FETCH):
+                n = min(FETCH, width - lo)
+                looked_up = window.indirect(entries(offsets, start + lo, n))
+                if on_vector:
+                    nc.vector.tensor_copy(out[:, lo : lo + n], looked_up)
+                else:
+                    nc.scalar.activation(out[:, lo : lo + n], looked_up, ACT.Copy)
+
+        def gate_argument(chunk, t):
+            start, width = MIX_CHUNKS[chunk]
+            if chunk == 0:
+                leave_b(t)
+            b_far = ring.tile([P, width], F32, name="b_far", tag="b_far", align_bytes=64, bufs=FAR_BUFS)
+            fetch(b_far, b_rows[t][:], n2_list, start, width, False)
+            gate = ring.tile([P, width], F32, name="gate", tag="gate", align_bytes=64, bufs=GATE_BUFS)
+            nc.vector.tensor_tensor(gate[:], b_far[:], b_rows[t][:, start : start + width], ALU.subtract)
+            return gate
+
+        def mix(chunk, t, gate):
+            start, width = MIX_CHUNKS[chunk]
+            cols = slice(start, start + width)
+            if chunk == 0:
+                leave_a(t)
+            step = ring.tile([P, width], F32, name="step", tag="step", align_bytes=64, bufs=STEP_BUFS)
+            fetch(step, a_rows[t][:], n1_list, start, width, (chunk, t) in N1_ON_VECTOR)
+            nc.scalar.activation(gate[:], gate[:], ACT.Tanh, scale=SCORE_SCALE / 2)
+            nc.vector.scalar_tensor_tensor(near[:, t, cols], gate[:], 1.0, a_rows[t][:, cols], ALU.subtract, ALU.mult)
+            nc.vector.scalar_tensor_tensor(far[:, t, cols], gate[:], 1.0, step[:], ALU.add, ALU.mult)
+
+        def weave(start, width):
+            nc.vector.tensor_tensor(
+                woven(z_woven, start, width), planar(far, start, width), planar(near, start, width), ALU.subtract
+            )
+
+        def last_product(start, width):
+            cols = slice(start, start + width)
+            nc.vector.quantize_mx(
+                out=z_words[:, cols].bitcast(FP8X4),
+                scales=z_scales[:, cols],
+                in_=z_woven[:, PACK * start : PACK * (start + width)],
+            )
+            for t in range(PACK):
+                product(h_banks[t][:, cols], w_words, w_scales, t, z_words[:, cols], z_scales[:, cols])
+
+        units = [(chunk, t) for chunk in range(len(MIX_CHUNKS)) for t in range(PACK)]
+        gates = {}
+        waiting = []
+        for turn in range(len(units) + LEAD):
+            if turn < len(units):
+                gates[turn] = gate_argument(*units[turn])
+            if turn >= LEAD:
+                chunk, t = units[turn - LEAD]
+                mix(chunk, t, gates[turn - LEAD])
+                if waiting:
+                    job, start, width = waiting[0]
+                    waiting = waiting[1:]
+                    job(start, width)
+                if t == PACK - 1:
+                    start, width = MIX_CHUNKS[chunk]
+                    waiting = waiting + [(weave, lo, PIECE) for lo in range(start, start + width, PIECE)]
+                    waiting = waiting + [(last_product, start, width)]
+        early = MIX_CHUNKS[-1][0]
+        h_rows = [new([P, S], F32, "h_rows%d" % t, ROW_TAGS[t]) for t in range(PACK)]
+        for t in H_ON_SCALAR:
+            nc.scalar.copy(h_rows[t][:, :early], h_banks[t][:, :early])
+        for job, start, width in waiting:
+            job(start, width)
+        nc.scalar.copy(h_rows[0][:, early:], h_banks[0][:, early:])
+        for t in range(1, PACK):
+            lo = early if t in H_ON_SCALAR else 0
+            nc.vector.tensor_copy(h_rows[t][:, lo:], h_banks[t][:, lo:])
+
+        result = new([P, PACK, S], F32, "result")
+        result_woven = new([P, PACK * S], BF16, "result_woven")
+        result_words = new([P, S], U32, "result_words")
+        result_scales = new([P, S], U8, "result_scales")
+        out_rows = out_0.rearrange("(p t) j -> p t j", t=PACK)
+        for start, width in OUT_CHUNKS:
+            cols = slice(start, start + width)
+            for t in range(PACK):
+                other = ring.tile([P, width], F32, name="other", tag="other", align_bytes=64, bufs=OTHER_BUFS)
+                nc.scalar.activation(other[:], h_rows[t][:].indirect(entries(n3_list, start, width)), ACT.Copy)
+                nc.vector.tensor_tensor(result[:, t, cols], other[:], h_rows[t][:, cols], ALU.max)
+            nc.sync.dma_start(out_rows[:, :, cols], result[:, :, cols])
+            nc.vector.tensor_copy(woven(result_woven, start, width), planar(result, start, width))
+            nc.vector.quantize_mx(
+                out=result_words[:, cols].bitcast(FP8X4),
+                scales=result_scales[:, cols],
+                in_=result_woven[:, PACK * start : PACK * (start + width)],
+            )
+            nc.sync.dma_start(words_in_hbm(out_1)[:, cols], result_words[:, cols].bitcast(I32))
+        for q in range(4):
+            queue = nc.scalar if q % 2 == 0 else nc.sync
+            queue.dma_start(
+                out_2[0, 4 * q : 4 * q + 4, :].bitcast(I32), result_scales[32 * q : 32 * q + 4, :].bitcast(I32)
+            )

@@ -17,23 +17,21 @@ ALU = mybir.AluOpType
 
 P = 128
 PACK = 4
+QUADRANT = 32
+BLOCK_ROWS = 8
 LIST_ROWS = 16
 SCORE_SCALE = 0.0625
-MIX_CHUNKS = ((0, 256), (256, 128), (384, 128))
-OUT_CHUNKS = ((0, 256), (256, 128), (384, 128))
-FETCH = 256
-B_ON_SCALAR = (0, 1, 2)
-A_ON_SCALAR = (0,)
-H_ON_SCALAR = (0, 1, 2, 3)
-GATE_BUFS = 4
-STEP_BUFS = 3
-OTHER_BUFS = 4
+LINE_BYTES = 16
+
+CHUNKS = ((0, 256), (256, 128), (384, 128))
+LAST_START = CHUNKS[-1][0]
+WEAVE_WIDTH = 128
+HALF = S // 2
+PLANES_IN_HALVES = 2
+B_PLANES_ON_SCALAR = (0, 1, 2)
+A_PLANES_ON_SCALAR = (0,)
 LEAD = 2
-N1_ON_VECTOR = ((0, 1),)
-D_ZERO_GPSIMD = False
-FAR_BUFS = 2
-PIECE = 128
-ROW_TAGS = ("rows0", "rows1", "x_scale_table", "x_word_table")
+B_FAR_BUFS, GATE_BUFS, HALF_FAR_BUFS, H_FAR_BUFS = 2, 4, 3, 4
 
 
 def entries(offsets, start, width):
@@ -71,10 +69,43 @@ def tile_picked_twkspullbbig_none_po_kernel(
         def new(shape, dtype, name, tag=None):
             return held.tile(shape, dtype, name=name, tag=tag or name, align_bytes=64)
 
+        def in_turn(width, name, bufs):
+            return ring.tile([P, width], F32, name=name, tag=name, align_bytes=64, bufs=bufs)
+
+        def bank(width, name, tag):
+            return psum.tile([P, width], F32, name=name, tag=tag)
+
         def load_list(source, name):
             offsets = new([P, S // LIST_ROWS], U16, name)
             nc.sync.dma_start(offsets[:], source)
             return offsets
+
+        def load_spread_scales(tile, scales):
+            nc.sync.dma_start(tile[0:P:BLOCK_ROWS, :].bitcast(I32), scales[0].bitcast(I32))
+
+        def place_scale_rows(placed, spread, r):
+            nc.sync.dma_start(
+                placed[r:P:QUADRANT, :].bitcast(I32), spread[BLOCK_ROWS * r : P : QUADRANT, :].bitcast(I32)
+            )
+
+        def product(out, lhs_words, lhs_scales, t, rhs_words, rhs_scales):
+            rows = slice(P * t, P * (t + 1))
+            nc.tensor.matmul_mx(
+                out=out,
+                lhsT=lhs_words[:, rows].bitcast(FP8X4),
+                lhsT_scale=lhs_scales[:, rows],
+                rhs=rhs_words.bitcast(FP8X4),
+                rhs_scale=rhs_scales,
+                start=True,
+                stop=True,
+            )
+
+        def quantise(words, scales, source, start, width):
+            nc.vector.quantize_mx(
+                out=words[:, start : start + width].bitcast(FP8X4),
+                scales=scales[:, start : start + width],
+                in_=source[:, PACK * start : PACK * (start + width)],
+            )
 
         d_scale_table = new([P, G], U8, "d_scale_table")
         x_scale_table = new([P, T], U8, "x_scale_table")
@@ -84,196 +115,173 @@ def tile_picked_twkspullbbig_none_po_kernel(
         w_scales_raw = new([P, N], U8, "w_scales_raw")
         w_words_raw = new([P, N], U32, "w_words_raw")
         gain = new([P, PACK], F32, "gain")
-
-        (nc.gpsimd if D_ZERO_GPSIMD else nc.vector).memset(d_scale_table[:].bitcast(I32), 0)
-        nc.vector.memset(x_scale_table[:].bitcast(I32), 0)
-        nc.vector.memset(key_scales[:].bitcast(I32), 0)
-        nc.gpsimd.memset(w_scales_raw[:].bitcast(I32), 0)
+        w_scales = new([P, N], U8, "w_scales")
+        for table in (d_scale_table, x_scale_table, key_scales, w_scales_raw, w_scales):
+            nc.vector.memset(table[:].bitcast(I32), 0)
 
         k1_list = load_list(k1, "k1_list")
         two_list = load_list(two, "two_list")
-        nc.sync.dma_start(d_scale_table[0:P:8, :].bitcast(I32), d_scales[0].bitcast(I32))
-        for q in range(4):
+        load_spread_scales(d_scale_table, d_scales)
+        for q in range(P // QUADRANT):
             queue = nc.scalar if q < 2 else nc.sync
             queue.dma_start(
-                x_scale_table[32 * q : 32 * q + 4, :].bitcast(I32), x_scales[0, 4 * q : 4 * q + 4, :].bitcast(I32)
+                x_scale_table[QUADRANT * q : QUADRANT * q + PACK, :].bitcast(I32),
+                x_scales[0, PACK * q : PACK * (q + 1), :].bitcast(I32),
             )
         nc.sync.dma_start(d_word_table[:].bitcast(I32), words_in_hbm(d_words))
         nc.sync.dma_start(x_word_table[:].bitcast(I32), words_in_hbm(x_words))
+        nc.sync.dma_start(gain[:], gn.rearrange("(p t) o -> p (t o)", t=PACK))
         n2_list = load_list(n2, "n2_list")
-        nc.gpsimd.dma_start(gain[:], gn.rearrange("(p t) o -> p (t o)", t=PACK))
-        for q in range(4):
-            nc.gpsimd.dma_start(
-                w_scales_raw[32 * q : 32 * q + 4, :].bitcast(I32), w1_scales[0, 4 * q : 4 * q + 4, :].bitcast(I32)
-            )
 
-        row_scale = new([P, PACK], F32, "row_scale")
-        nc.scalar.activation(row_scale[:], gain[:], ACT.Copy, scale=SCORE_SCALE / 2)
+        half_scale = new([P, PACK], F32, "half_scale")
+        nc.scalar.activation(half_scale[:], gain[:], ACT.Copy, scale=SCORE_SCALE / 2)
 
         picked_d_scales = new([P, H], U8, "picked_d_scales")
         dealt_d_scales = new([P, H], U8, "dealt_d_scales")
         nc.vector.tensor_copy(picked_d_scales[:], d_scale_table[:].indirect(k1_list[:]))
-        nc.vector.tensor_copy(*dealt_views(dealt_d_scales[:], picked_d_scales[:], 16))
-        for r in range(4):
-            nc.sync.dma_start(key_scales[r:P:32, :].bitcast(I32), dealt_d_scales[8 * r : P : 32, :].bitcast(I32))
-        n1_list = load_list(n1, "n1_list")
+        nc.vector.tensor_copy(*dealt_views(dealt_d_scales[:], picked_d_scales[:], LINE_BYTES))
+        place_scale_rows(key_scales, dealt_d_scales, 0)
+        place_scale_rows(key_scales, dealt_d_scales, 1)
         offs_list = load_list(offs, "offs_list")
+        place_scale_rows(key_scales, dealt_d_scales, 2)
+        place_scale_rows(key_scales, dealt_d_scales, 3)
         nc.sync.dma_start(w_words_raw[:].bitcast(I32), words_in_hbm(w1_words))
+        load_spread_scales(w_scales_raw, w1_scales)
+        n1_list = load_list(n1, "n1_list")
         n3_list = load_list(n3, "n3_list")
+
+        def scores(offsets, scales, name, side):
+            words = new([P, S], U32, name + "_words")
+            banks = [bank(S, name + "_bank%d" % t, side % t) for t in range(PACK)]
+            for start in (0, HALF):
+                cols = slice(start, start + HALF)
+                nc.vector.tensor_copy(words[:, cols], x_word_table[:].indirect(entries(offsets, start, HALF)))
+                for t in range(PLANES_IN_HALVES):
+                    product(banks[t][:, cols], key_words, key_scales, t, words[:, cols], scales[:, cols])
+            for t in range(PLANES_IN_HALVES, PACK):
+                product(banks[t][:], key_words, key_scales, t, words[:], scales[:])
+            return banks
 
         two_scales = new([P, S], U8, "two_scales")
         nc.vector.tensor_copy(two_scales[:], x_scale_table[:].indirect(two_list[:]))
         picked_d_words = new([P, H], U32, "picked_d_words")
         key_words = new([P, H], U32, "key_words")
         nc.vector.tensor_copy(picked_d_words[:], d_word_table[:].indirect(k1_list[:]))
-        nc.vector.tensor_copy(*dealt_views(key_words[:], picked_d_words[:], 4))
-        two_words = new([P, S], U32, "two_words")
-        nc.vector.tensor_copy(two_words[:], x_word_table[:].indirect(two_list[:]))
-
-        def product(bank, lhs_words, lhs_scales, t, rhs_words, rhs_scales):
-            rows = slice(P * t, P * (t + 1))
-            nc.tensor.matmul_mx(
-                out=bank,
-                lhsT=lhs_words[:, rows].bitcast(FP8X4),
-                lhsT_scale=lhs_scales[:, rows],
-                rhs=rhs_words.bitcast(FP8X4),
-                rhs_scale=rhs_scales,
-                start=True,
-                stop=True,
-            )
-
-        b_banks = [psum.tile([P, S], F32, name="b_bank%d" % t, tag="low%d" % t) for t in range(PACK)]
-        for t in range(PACK):
-            product(b_banks[t][:], key_words, key_scales, t, two_words[:], two_scales[:])
-
+        nc.vector.tensor_copy(*dealt_views(key_words[:], picked_d_words[:], LINE_BYTES // 4))
+        b_banks = scores(two_list, two_scales, "b", "low%d")
         offs_scales = new([P, S], U8, "offs_scales")
-        offs_words = new([P, S], U32, "offs_words")
         nc.vector.tensor_copy(offs_scales[:], x_scale_table[:].indirect(offs_list[:]))
-        nc.vector.tensor_copy(offs_words[:], x_word_table[:].indirect(offs_list[:]))
-        a_banks = [psum.tile([P, S], F32, name="a_bank%d" % t, tag="high%d" % t) for t in range(PACK)]
-        for t in range(PACK):
-            product(a_banks[t][:], key_words, key_scales, t, offs_words[:], offs_scales[:])
+        a_banks = scores(offs_list, offs_scales, "a", "high%d")
 
         w_words = new([P, N], U32, "w_words")
-        w_scales = new([P, N], U8, "w_scales")
-        nc.gpsimd.tensor_copy(*dealt_views(w_words[:], w_words_raw[:], 4))
-        nc.gpsimd.tensor_copy(*dealt_views(w_scales[:], w_scales_raw[:], 16))
+        dealt_w_scales = new([P, N], U8, "dealt_w_scales", "x_scale_table")
+        nc.vector.tensor_copy(*dealt_views(w_words[:], w_words_raw[:], LINE_BYTES // 4))
+        nc.vector.tensor_copy(*dealt_views(dealt_w_scales[:], w_scales_raw[:], LINE_BYTES))
+        for r in range(PACK):
+            place_scale_rows(w_scales, dealt_w_scales, r)
 
-        b_rows = [new([P, S], F32, "b_rows%d" % t, ROW_TAGS[t]) for t in range(PACK)]
-        a_rows = [new([P, S], F32, "a_rows%d" % t) for t in range(PACK)]
-        far = new([P, PACK, S], F32, "far")
-        near = new([P, PACK, S], F32, "near")
+        b_rows = [
+            new([P, S], F32, "b_rows%d" % t, None if t in B_PLANES_ON_SCALAR else "x_word_table") for t in range(PACK)
+        ]
+        half_rows = [new([P, S], F32, "half_rows%d" % t) for t in range(PACK)]
+        far_term = new([P, PACK, S], F32, "far_term")
+        near_term = new([P, PACK, S], F32, "near_term")
         z_woven = new([P, PACK * S], BF16, "z_woven")
         z_words = new([P, S], U32, "z_words")
         z_scales = new([P, S], U8, "z_scales")
-        h_banks = [psum.tile([P, S], F32, name="h_bank%d" % t, tag="low%d" % t) for t in range(PACK)]
+        early_banks = [bank(LAST_START, "early_bank%d" % t, "high%d" % t) for t in range(PACK)]
+        late_banks = [bank(S - LAST_START, "late_bank%d" % t, "low%d" % t) for t in range(PACK)]
 
-        def leave_b(t):
-            if t in B_ON_SCALAR:
-                nc.scalar.copy(b_rows[t][:], b_banks[t][:])
-            else:
-                nc.vector.tensor_copy(b_rows[t][:], b_banks[t][:])
-
-        def leave_a(t):
-            if t in A_ON_SCALAR:
-                nc.scalar.activation(a_rows[t][:], a_banks[t][:], ACT.Copy, scale=row_scale[:, t : t + 1])
-            else:
-                nc.vector.tensor_scalar(a_rows[t][:], a_banks[t][:], row_scale[:, t : t + 1], None, ALU.mult)
-
-        def fetch(out, window, offsets, start, width, on_vector):
-            for lo in range(0, width, FETCH):
-                n = min(FETCH, width - lo)
-                looked_up = window.indirect(entries(offsets, start + lo, n))
-                if on_vector:
-                    nc.vector.tensor_copy(out[:, lo : lo + n], looked_up)
+        def gate_argument(start, width, t):
+            if start == 0:
+                if t in B_PLANES_ON_SCALAR:
+                    nc.scalar.copy(b_rows[t][:], b_banks[t][:])
                 else:
-                    nc.scalar.activation(out[:, lo : lo + n], looked_up, ACT.Copy)
-
-        def gate_argument(chunk, t):
-            start, width = MIX_CHUNKS[chunk]
-            if chunk == 0:
-                leave_b(t)
-            b_far = ring.tile([P, width], F32, name="b_far", tag="b_far", align_bytes=64, bufs=FAR_BUFS)
-            fetch(b_far, b_rows[t][:], n2_list, start, width, False)
-            gate = ring.tile([P, width], F32, name="gate", tag="gate", align_bytes=64, bufs=GATE_BUFS)
+                    nc.vector.tensor_copy(b_rows[t][:], b_banks[t][:])
+            b_far = in_turn(width, "b_far", B_FAR_BUFS)
+            nc.scalar.activation(b_far[:], b_rows[t][:].indirect(entries(n2_list, start, width)), ACT.Copy)
+            gate = in_turn(width, "gate", GATE_BUFS)
             nc.vector.tensor_tensor(gate[:], b_far[:], b_rows[t][:, start : start + width], ALU.subtract)
             return gate
 
-        def mix(chunk, t, gate):
-            start, width = MIX_CHUNKS[chunk]
+        def mix(start, width, t, gate):
             cols = slice(start, start + width)
-            if chunk == 0:
-                leave_a(t)
-            step = ring.tile([P, width], F32, name="step", tag="step", align_bytes=64, bufs=STEP_BUFS)
-            fetch(step, a_rows[t][:], n1_list, start, width, (chunk, t) in N1_ON_VECTOR)
             nc.scalar.activation(gate[:], gate[:], ACT.Tanh, scale=SCORE_SCALE / 2)
-            nc.vector.scalar_tensor_tensor(near[:, t, cols], gate[:], 1.0, a_rows[t][:, cols], ALU.subtract, ALU.mult)
-            nc.vector.scalar_tensor_tensor(far[:, t, cols], gate[:], 1.0, step[:], ALU.add, ALU.mult)
+            if start == 0:
+                if t in A_PLANES_ON_SCALAR:
+                    nc.scalar.activation(half_rows[t][:], a_banks[t][:], ACT.Copy, scale=half_scale[:, t : t + 1])
+                else:
+                    nc.vector.tensor_scalar(half_rows[t][:], a_banks[t][:], half_scale[:, t : t + 1], None, ALU.mult)
+            half_far = in_turn(width, "half_far", HALF_FAR_BUFS)
+            looked_up = half_rows[t][:].indirect(entries(n1_list, start, width))
+            if start == 0 and t % 2 == 1:
+                nc.vector.tensor_copy(half_far[:], looked_up)
+            else:
+                nc.scalar.activation(half_far[:], looked_up, ACT.Copy)
+            nc.vector.scalar_tensor_tensor(
+                near_term[:, t, cols], gate[:], 1.0, half_rows[t][:, cols], ALU.subtract, ALU.mult
+            )
+            nc.vector.scalar_tensor_tensor(far_term[:, t, cols], gate[:], 1.0, half_far[:], ALU.add, ALU.mult)
 
-        def weave(start, width):
+        def weave_z(start, width):
             nc.vector.tensor_tensor(
-                woven(z_woven, start, width), planar(far, start, width), planar(near, start, width), ALU.subtract
+                woven(z_woven, start, width),
+                planar(far_term, start, width),
+                planar(near_term, start, width),
+                ALU.subtract,
             )
 
-        def last_product(start, width):
+        def layer(start, width):
             cols = slice(start, start + width)
-            nc.vector.quantize_mx(
-                out=z_words[:, cols].bitcast(FP8X4),
-                scales=z_scales[:, cols],
-                in_=z_woven[:, PACK * start : PACK * (start + width)],
-            )
+            quantise(z_words, z_scales, z_woven, start, width)
             for t in range(PACK):
-                product(h_banks[t][:, cols], w_words, w_scales, t, z_words[:, cols], z_scales[:, cols])
+                out = early_banks[t][:, cols] if start < LAST_START else late_banks[t][:]
+                product(out, w_words, w_scales, t, z_words[:, cols], z_scales[:, cols])
 
-        units = [(chunk, t) for chunk in range(len(MIX_CHUNKS)) for t in range(PACK)]
-        gates = {}
+        units = [(start, width, t) for start, width in CHUNKS for t in range(PACK)]
+        gates = []
         waiting = []
         for turn in range(len(units) + LEAD):
             if turn < len(units):
-                gates[turn] = gate_argument(*units[turn])
+                gates.append(gate_argument(*units[turn]))
             if turn >= LEAD:
-                chunk, t = units[turn - LEAD]
-                mix(chunk, t, gates[turn - LEAD])
+                start, width, t = units[turn - LEAD]
+                mix(start, width, t, gates[turn - LEAD])
                 if waiting:
-                    job, start, width = waiting[0]
+                    step, first, columns = waiting[0]
                     waiting = waiting[1:]
-                    job(start, width)
+                    step(first, columns)
                 if t == PACK - 1:
-                    start, width = MIX_CHUNKS[chunk]
-                    waiting = waiting + [(weave, lo, PIECE) for lo in range(start, start + width, PIECE)]
-                    waiting = waiting + [(last_product, start, width)]
-        early = MIX_CHUNKS[-1][0]
-        h_rows = [new([P, S], F32, "h_rows%d" % t, ROW_TAGS[t]) for t in range(PACK)]
-        for t in H_ON_SCALAR:
-            nc.scalar.copy(h_rows[t][:, :early], h_banks[t][:, :early])
-        for job, start, width in waiting:
-            job(start, width)
-        nc.scalar.copy(h_rows[0][:, early:], h_banks[0][:, early:])
-        for t in range(1, PACK):
-            lo = early if t in H_ON_SCALAR else 0
-            nc.vector.tensor_copy(h_rows[t][:, lo:], h_banks[t][:, lo:])
+                    waiting = waiting + [(weave_z, lo, WEAVE_WIDTH) for lo in range(start, start + width, WEAVE_WIDTH)]
+                    waiting = waiting + [(layer, start, width)]
+        h_rows = [new([P, S], F32, "h_rows%d" % t) for t in range(PACK)]
+        for t in range(PACK):
+            nc.scalar.copy(h_rows[t][:, :LAST_START], early_banks[t][:])
+        for step, first, columns in waiting:
+            step(first, columns)
+        for t in range(PACK):
+            nc.vector.tensor_copy(h_rows[t][:, LAST_START:], late_banks[t][:])
 
         result = new([P, PACK, S], F32, "result")
         result_woven = new([P, PACK * S], BF16, "result_woven")
         result_words = new([P, S], U32, "result_words")
         result_scales = new([P, S], U8, "result_scales")
         out_rows = out_0.rearrange("(p t) j -> p t j", t=PACK)
-        for start, width in OUT_CHUNKS:
+        for start, width in CHUNKS:
             cols = slice(start, start + width)
             for t in range(PACK):
-                other = ring.tile([P, width], F32, name="other", tag="other", align_bytes=64, bufs=OTHER_BUFS)
-                nc.scalar.activation(other[:], h_rows[t][:].indirect(entries(n3_list, start, width)), ACT.Copy)
-                nc.vector.tensor_tensor(result[:, t, cols], other[:], h_rows[t][:, cols], ALU.max)
+                h_far = in_turn(width, "h_far", H_FAR_BUFS)
+                nc.scalar.activation(h_far[:], h_rows[t][:].indirect(entries(n3_list, start, width)), ACT.Copy)
+                nc.vector.tensor_tensor(result[:, t, cols], h_far[:], h_rows[t][:, cols], ALU.max)
             nc.sync.dma_start(out_rows[:, :, cols], result[:, :, cols])
             nc.vector.tensor_copy(woven(result_woven, start, width), planar(result, start, width))
-            nc.vector.quantize_mx(
-                out=result_words[:, cols].bitcast(FP8X4),
-                scales=result_scales[:, cols],
-                in_=result_woven[:, PACK * start : PACK * (start + width)],
-            )
-            nc.sync.dma_start(words_in_hbm(out_1)[:, cols], result_words[:, cols].bitcast(I32))
-        for q in range(4):
+            quantise(result_words, result_scales, result_woven, start, width)
+            if start + width >= LAST_START:
+                done = slice(0, LAST_START) if start < LAST_START else cols
+                nc.sync.dma_start(words_in_hbm(out_1)[:, done], result_words[:, done].bitcast(I32))
+        for q in range(P // QUADRANT):
             queue = nc.scalar if q % 2 == 0 else nc.sync
             queue.dma_start(
-                out_2[0, 4 * q : 4 * q + 4, :].bitcast(I32), result_scales[32 * q : 32 * q + 4, :].bitcast(I32)
+                out_2[0, PACK * q : PACK * (q + 1), :].bitcast(I32),
+                result_scales[QUADRANT * q : QUADRANT * q + PACK, :].bitcast(I32),
             )

from contextlib import ExitStack

import concourse.mybir as mybir

K, T, S, N, G, H = 512, 2048, 512, 512, 2048, 512
FLOPS = 2 * K * H * S * 2 + 2 * H * N * S

F32 = mybir.dt.float32
BF16 = mybir.dt.bfloat16
I32 = mybir.dt.int32
U32 = mybir.dt.uint32
U16 = mybir.dt.uint16
U8 = mybir.dt.uint8
FP8X4 = mybir.dt.float8_e4m3fn_x4
ACT = mybir.ActivationFunctionType
ALU = mybir.AluOpType

P = 128
PACK = 4
QUADRANT = 32
BLOCK_ROWS = 8
LIST_ROWS = 16
SCORE_SCALE = 0.0625
LINE_BYTES = 16

CHUNKS = ((0, 256), (256, 128), (384, 128))
LAST_START = CHUNKS[-1][0]
WEAVE_WIDTH = 128
HALF = S // 2
PLANES_IN_HALVES = 2
B_PLANES_ON_SCALAR = (0, 1, 2)
A_PLANES_ON_SCALAR = (0,)
LEAD = 2
B_FAR_BUFS, GATE_BUFS, HALF_FAR_BUFS, H_FAR_BUFS = 2, 4, 3, 4


def entries(offsets, start, width):
    return offsets[:, start // LIST_ROWS : (start + width) // LIST_ROWS]


def words_in_hbm(words):
    return words[0].rearrange("p n t -> p (n t)").bitcast(I32)


def dealt_views(dst, src, run):
    return (
        dst.rearrange("p (t c i) -> p c t i", t=PACK, i=run),
        src.rearrange("p (c i t) -> p c t i", t=PACK, i=run),
    )


def woven(tile, start, width):
    return tile[:, PACK * start : PACK * (start + width)].rearrange("p (c i t) -> p c t i", t=PACK, i=PACK)


def planar(tile, start, width):
    return tile[:, :, start : start + width].rearrange("p t (c i) -> p c t i", i=PACK)


def tile_picked_twkspullbbig_none_po_kernel(
    tc, x_words, x_scales, d_words, d_scales, gn, w1_words, w1_scales, offs, k1, two, n1, n2, n3, out_0, out_1, out_2
):
    nc = tc.nc
    with ExitStack() as ctx:
        held = ctx.enter_context(tc.tile_pool(name="held", bufs=1))
        ring = ctx.enter_context(tc.tile_pool(name="ring", bufs=3))
        psum = ctx.enter_context(tc.psum_pool(name="psum", bufs=1))

        def new(shape, dtype, name, tag=None):
            return held.tile(shape, dtype, name=name, tag=tag or name, align_bytes=64)

        def in_turn(width, name, bufs):
            return ring.tile([P, width], F32, name=name, tag=name, align_bytes=64, bufs=bufs)

        def bank(width, name, tag):
            return psum.tile([P, width], F32, name=name, tag=tag)

        def load_list(source, name):
            offsets = new([P, S // LIST_ROWS], U16, name)
            nc.sync.dma_start(offsets[:], source)
            return offsets

        def load_spread_scales(tile, scales):
            nc.sync.dma_start(tile[0:P:BLOCK_ROWS, :].bitcast(I32), scales[0].bitcast(I32))

        def place_scale_rows(placed, spread, r):
            nc.sync.dma_start(
                placed[r:P:QUADRANT, :].bitcast(I32), spread[BLOCK_ROWS * r : P : QUADRANT, :].bitcast(I32)
            )

        def product(out, lhs_words, lhs_scales, t, rhs_words, rhs_scales):
            rows = slice(P * t, P * (t + 1))
            nc.tensor.matmul_mx(
                out=out,
                lhsT=lhs_words[:, rows].bitcast(FP8X4),
                lhsT_scale=lhs_scales[:, rows],
                rhs=rhs_words.bitcast(FP8X4),
                rhs_scale=rhs_scales,
                start=True,
                stop=True,
            )

        def quantise(words, scales, source, start, width):
            nc.vector.quantize_mx(
                out=words[:, start : start + width].bitcast(FP8X4),
                scales=scales[:, start : start + width],
                in_=source[:, PACK * start : PACK * (start + width)],
            )

        d_scale_table = new([P, G], U8, "d_scale_table")
        x_scale_table = new([P, T], U8, "x_scale_table")
        d_word_table = new([P, G], U32, "d_word_table")
        x_word_table = new([P, T], U32, "x_word_table")
        key_scales = new([P, H], U8, "key_scales")
        w_scales_raw = new([P, N], U8, "w_scales_raw")
        w_words_raw = new([P, N], U32, "w_words_raw")
        gain = new([P, PACK], F32, "gain")
        w_scales = new([P, N], U8, "w_scales")
        for table in (d_scale_table, x_scale_table, key_scales, w_scales_raw, w_scales):
            nc.vector.memset(table[:].bitcast(I32), 0)

        k1_list = load_list(k1, "k1_list")
        two_list = load_list(two, "two_list")
        load_spread_scales(d_scale_table, d_scales)
        for q in range(P // QUADRANT):
            queue = nc.scalar if q < 2 else nc.sync
            queue.dma_start(
                x_scale_table[QUADRANT * q : QUADRANT * q + PACK, :].bitcast(I32),
                x_scales[0, PACK * q : PACK * (q + 1), :].bitcast(I32),
            )
        nc.sync.dma_start(d_word_table[:].bitcast(I32), words_in_hbm(d_words))
        nc.sync.dma_start(x_word_table[:].bitcast(I32), words_in_hbm(x_words))
        nc.sync.dma_start(gain[:], gn.rearrange("(p t) o -> p (t o)", t=PACK))
        n2_list = load_list(n2, "n2_list")

        half_scale = new([P, PACK], F32, "half_scale")
        nc.scalar.activation(half_scale[:], gain[:], ACT.Copy, scale=SCORE_SCALE / 2)

        picked_d_scales = new([P, H], U8, "picked_d_scales")
        dealt_d_scales = new([P, H], U8, "dealt_d_scales")
        nc.vector.tensor_copy(picked_d_scales[:], d_scale_table[:].indirect(k1_list[:]))
        nc.vector.tensor_copy(*dealt_views(dealt_d_scales[:], picked_d_scales[:], LINE_BYTES))
        place_scale_rows(key_scales, dealt_d_scales, 0)
        place_scale_rows(key_scales, dealt_d_scales, 1)
        offs_list = load_list(offs, "offs_list")
        place_scale_rows(key_scales, dealt_d_scales, 2)
        place_scale_rows(key_scales, dealt_d_scales, 3)
        nc.sync.dma_start(w_words_raw[:].bitcast(I32), words_in_hbm(w1_words))
        load_spread_scales(w_scales_raw, w1_scales)
        n1_list = load_list(n1, "n1_list")
        n3_list = load_list(n3, "n3_list")

        def scores(offsets, scales, name, side):
            words = new([P, S], U32, name + "_words")
            banks = [bank(S, name + "_bank%d" % t, side % t) for t in range(PACK)]
            for start in (0, HALF):
                cols = slice(start, start + HALF)
                nc.vector.tensor_copy(words[:, cols], x_word_table[:].indirect(entries(offsets, start, HALF)))
                for t in range(PLANES_IN_HALVES):
                    product(banks[t][:, cols], key_words, key_scales, t, words[:, cols], scales[:, cols])
            for t in range(PLANES_IN_HALVES, PACK):
                product(banks[t][:], key_words, key_scales, t, words[:], scales[:])
            return banks

        two_scales = new([P, S], U8, "two_scales")
        nc.vector.tensor_copy(two_scales[:], x_scale_table[:].indirect(two_list[:]))
        picked_d_words = new([P, H], U32, "picked_d_words")
        key_words = new([P, H], U32, "key_words")
        nc.vector.tensor_copy(picked_d_words[:], d_word_table[:].indirect(k1_list[:]))
        nc.vector.tensor_copy(*dealt_views(key_words[:], picked_d_words[:], LINE_BYTES // 4))
        b_banks = scores(two_list, two_scales, "b", "low%d")
        offs_scales = new([P, S], U8, "offs_scales")
        nc.vector.tensor_copy(offs_scales[:], x_scale_table[:].indirect(offs_list[:]))
        a_banks = scores(offs_list, offs_scales, "a", "high%d")

        w_words = new([P, N], U32, "w_words")
        dealt_w_scales = new([P, N], U8, "dealt_w_scales", "x_scale_table")
        nc.vector.tensor_copy(*dealt_views(w_words[:], w_words_raw[:], LINE_BYTES // 4))
        nc.vector.tensor_copy(*dealt_views(dealt_w_scales[:], w_scales_raw[:], LINE_BYTES))
        for r in range(PACK):
            place_scale_rows(w_scales, dealt_w_scales, r)

        b_rows = [
            new([P, S], F32, "b_rows%d" % t, None if t in B_PLANES_ON_SCALAR else "x_word_table") for t in range(PACK)
        ]
        half_rows = [new([P, S], F32, "half_rows%d" % t) for t in range(PACK)]
        far_term = new([P, PACK, S], F32, "far_term")
        near_term = new([P, PACK, S], F32, "near_term")
        z_woven = new([P, PACK * S], BF16, "z_woven")
        z_words = new([P, S], U32, "z_words")
        z_scales = new([P, S], U8, "z_scales")
        early_banks = [bank(LAST_START, "early_bank%d" % t, "high%d" % t) for t in range(PACK)]
        late_banks = [bank(S - LAST_START, "late_bank%d" % t, "low%d" % t) for t in range(PACK)]

        def gate_argument(start, width, t):
            if start == 0:
                if t in B_PLANES_ON_SCALAR:
                    nc.scalar.copy(b_rows[t][:], b_banks[t][:])
                else:
                    nc.vector.tensor_copy(b_rows[t][:], b_banks[t][:])
            b_far = in_turn(width, "b_far", B_FAR_BUFS)
            nc.scalar.activation(b_far[:], b_rows[t][:].indirect(entries(n2_list, start, width)), ACT.Copy)
            gate = in_turn(width, "gate", GATE_BUFS)
            nc.vector.tensor_tensor(gate[:], b_far[:], b_rows[t][:, start : start + width], ALU.subtract)
            return gate

        def mix(start, width, t, gate):
            cols = slice(start, start + width)
            nc.scalar.activation(gate[:], gate[:], ACT.Tanh, scale=SCORE_SCALE / 2)
            if start == 0:
                if t in A_PLANES_ON_SCALAR:
                    nc.scalar.activation(half_rows[t][:], a_banks[t][:], ACT.Copy, scale=half_scale[:, t : t + 1])
                else:
                    nc.vector.tensor_scalar(half_rows[t][:], a_banks[t][:], half_scale[:, t : t + 1], None, ALU.mult)
            half_far = in_turn(width, "half_far", HALF_FAR_BUFS)
            looked_up = half_rows[t][:].indirect(entries(n1_list, start, width))
            if start == 0 and t % 2 == 1:
                nc.vector.tensor_copy(half_far[:], looked_up)
            else:
                nc.scalar.activation(half_far[:], looked_up, ACT.Copy)
            nc.vector.scalar_tensor_tensor(
                near_term[:, t, cols], gate[:], 1.0, half_rows[t][:, cols], ALU.subtract, ALU.mult
            )
            nc.vector.scalar_tensor_tensor(far_term[:, t, cols], gate[:], 1.0, half_far[:], ALU.add, ALU.mult)

        def weave_z(start, width):
            nc.vector.tensor_tensor(
                woven(z_woven, start, width),
                planar(far_term, start, width),
                planar(near_term, start, width),
                ALU.subtract,
            )

        def layer(start, width):
            cols = slice(start, start + width)
            quantise(z_words, z_scales, z_woven, start, width)
            for t in range(PACK):
                out = early_banks[t][:, cols] if start < LAST_START else late_banks[t][:]
                product(out, w_words, w_scales, t, z_words[:, cols], z_scales[:, cols])

        units = [(start, width, t) for start, width in CHUNKS for t in range(PACK)]
        gates = []
        waiting = []
        for turn in range(len(units) + LEAD):
            if turn < len(units):
                gates.append(gate_argument(*units[turn]))
            if turn >= LEAD:
                start, width, t = units[turn - LEAD]
                mix(start, width, t, gates[turn - LEAD])
                if waiting:
                    step, first, columns = waiting[0]
                    waiting = waiting[1:]
                    step(first, columns)
                if t == PACK - 1:
                    waiting = waiting + [(weave_z, lo, WEAVE_WIDTH) for lo in range(start, start + width, WEAVE_WIDTH)]
                    waiting = waiting + [(layer, start, width)]
        h_rows = [new([P, S], F32, "h_rows%d" % t) for t in range(PACK)]
        for t in range(PACK):
            nc.scalar.copy(h_rows[t][:, :LAST_START], early_banks[t][:])
        for step, first, columns in waiting:
            step(first, columns)
        for t in range(PACK):
            nc.vector.tensor_copy(h_rows[t][:, LAST_START:], late_banks[t][:])

        result = new([P, PACK, S], F32, "result")
        result_woven = new([P, PACK * S], BF16, "result_woven")
        result_words = new([P, S], U32, "result_words")
        result_scales = new([P, S], U8, "result_scales")
        out_rows = out_0.rearrange("(p t) j -> p t j", t=PACK)
        for start, width in CHUNKS:
            cols = slice(start, start + width)
            for t in range(PACK):
                h_far = in_turn(width, "h_far", H_FAR_BUFS)
                nc.scalar.activation(h_far[:], h_rows[t][:].indirect(entries(n3_list, start, width)), ACT.Copy)
                nc.vector.tensor_tensor(result[:, t, cols], h_far[:], h_rows[t][:, cols], ALU.max)
            nc.sync.dma_start(out_rows[:, :, cols], result[:, :, cols])
            nc.vector.tensor_copy(woven(result_woven, start, width), planar(result, start, width))
            quantise(result_words, result_scales, result_woven, start, width)
            if start + width >= LAST_START:
                done = slice(0, LAST_START) if start < LAST_START else cols
                nc.sync.dma_start(words_in_hbm(out_1)[:, done], result_words[:, done].bitcast(I32))
        for q in range(P // QUADRANT):
            queue = nc.scalar if q % 2 == 0 else nc.sync
            queue.dma_start(
                out_2[0, PACK * q : PACK * (q + 1), :].bitcast(I32),
                result_scales[QUADRANT * q : QUADRANT * q + PACK, :].bitcast(I32),
            )
